import numpy as np
import ml_dtypes


def mxq(x, axis, fmt="e4m3"):
    dtype, down = {"e4m3": (ml_dtypes.float8_e4m3fn, 7), "e5m2": (ml_dtypes.float8_e5m2, 14)}[fmt]
    v = np.moveaxis(np.asarray(x, np.float32).astype(ml_dtypes.bfloat16).astype(np.float64), axis, -1)
    blocks = v.reshape(v.shape[:-1] + (-1, 32))
    amax = np.abs(blocks).max(-1, keepdims=True)
    byte = np.maximum(np.where(amax > 0, np.frexp(amax)[1] - 1 + 127, 0) - down, 1)
    scale = np.exp2(byte - 127.0)
    codes = (blocks / scale).astype(np.float32).astype(dtype).astype(np.float64)
    return np.moveaxis((codes * scale).reshape(v.shape), -1, axis)


WIDE = False


def mx_kscale(k):
    if not WIDE:
        return np.ones(k)
    levels = np.array([10, -10, 5, -5, 0])
    if k % 512:
        return np.exp2(np.random.permutation(np.resize(levels, k // 32))).repeat(32)
    a = np.empty((k // 512, 16))
    for p in range(k // 512):
        a[p, :8] = np.random.permutation(np.resize(levels, 8))
        for g in range(8):
            far = levels[np.abs(levels - a[p, g]) >= 10]
            a[p, g + 8] = far[np.random.randint(len(far))]
    return np.exp2(a.ravel()).repeat(32)


BF16 = ml_dtypes.bfloat16


def bf(x):
    return np.asarray(x, np.float32).astype(BF16)


def f64(x):
    return np.asarray(x).astype(np.float64)


E2M1 = np.array([0.0, 0.5, 1.0, 1.5, 2.0, 3.0, 4.0, 6.0, -0.0, -0.5, -1.0, -1.5, -2.0, -3.0, -4.0, -6.0])


def pack_weight(w, fmt):
    k, n = w.shape
    w = f64(bf(w)).reshape(k // 32, 32, n)
    amax = np.abs(w).max(1)
    if fmt == "e4m3":
        byte = np.frexp(amax)[1] - 1 + 127 - 7
    else:
        mant, ex = np.frexp(amax / 6.0)
        byte = np.where(mant > 0.5, ex, ex - 1) + 127
    byte = np.clip(np.where(amax > 0, byte, 1), 1, 254)
    scaled = (w * np.exp2(127.0 - byte)[:, None, :]).reshape(k, n).astype(np.float32)
    by_word = np.ascontiguousarray(scaled.reshape(k // 512, 128, 4, n).transpose(0, 1, 3, 2))
    if fmt == "e4m3":
        words = by_word.astype(ml_dtypes.float8_e4m3fn).view(np.uint8)
    else:
        c = by_word.astype(ml_dtypes.float4_e2m1fn).view(np.uint8) & 0xF
        words = c[..., 0::2] | (c[..., 1::2] << 4)
    return np.ascontiguousarray(words), np.ascontiguousarray(byte.astype(np.uint8).reshape(k // 512, 16, n))


def unpack_weight(words, scales, fmt):
    g, p, n, _ = words.shape
    if fmt == "e4m3":
        vals = np.ascontiguousarray(words).view(ml_dtypes.float8_e4m3fn).astype(np.float64)
    else:
        nib = np.empty((g, p, n, 4), np.uint8)
        nib[..., 0::2] = words & 0xF
        nib[..., 1::2] = words >> 4
        vals = E2M1[nib]
    vals = vals * np.repeat(np.exp2(scales.astype(np.float64) - 127.0), 8, axis=1)[..., None]
    return vals.transpose(0, 1, 3, 2).reshape(g * 512, n)
def pack4(w):
    words, scales = pack_weight(w, "e2m1")
    return words.reshape(words.shape[0], 128, -1), scales


def unpack4(words, scales):
    return unpack_weight(words.reshape(words.shape[0], 128, -1, 2), scales, "e2m1")


def planes(Y):
    n, m = Y.shape
    b = f64(bf(Y)).reshape(n // 32, 32, m)
    amax = np.abs(b).max(1)
    byte = np.clip(np.where(amax > 0, np.frexp(amax)[1] - 1 + 127 - 7, 1), 1, 254)
    codes = (b * np.exp2(127.0 - byte)[:, None, :]).reshape(n, m).astype(np.float32).astype(ml_dtypes.float8_e4m3fn).view(np.uint8)
    words = codes.reshape(n // 512, 128, 4, m).transpose(0, 1, 3, 2)
    return np.ascontiguousarray(words), np.ascontiguousarray(byte.astype(np.uint8).reshape(n // 512, 16, m))


N, M, D, F = 1024, 1024, 512, 1024


def hidden_sensitivity(inp_q, w, b, v):
    t = np.tanh((inp_q @ w) + f64(b))
    return (1.0 - t * t) * f64(v)


def setup_inputs():
    s, u = mx_kscale(D), mx_kscale(F)
    x = bf(np.random.standard_normal((N, D)) * s)
    y = bf(np.random.standard_normal((M, D)) / s)
    wa_words, wa_scales = pack4(np.random.standard_normal((D, F)) / np.sqrt(D) / s[:, None])
    wb_words, wb_scales = pack4(np.random.standard_normal((D, F)) / np.sqrt(D) * s[:, None])
    return {
        "x": x,
        "y": y,
        "wa_words": wa_words,
        "wa_scales": wa_scales,
        "wb_words": wb_words,
        "wb_scales": wb_scales,
        "b": bf(0.5 * np.random.standard_normal(F)),
        "va": bf(np.random.standard_normal(F) * u),
        "vb": bf(np.random.standard_normal(F) / u),
    }


def core(x, y, wa_words, wa_scales, wb_words, wb_scales, b, va, vb):
    d = x.shape[1]
    f = wa_scales.shape[2]
    xq = mxq(f64(x), 1, "e4m3")
    yq = mxq(f64(y), 1, "e4m3")
    da = hidden_sensitivity(xq, unpack4(wa_words, wa_scales), b, va)
    db = hidden_sensitivity(yq, unpack4(wb_words, wb_scales), b, vb)
    gram = (mxq(da, 1, "e4m3") @ mxq(db, 1, "e4m3").T) / np.sqrt(f)
    base = (xq @ yq.T) / np.sqrt(d)
    return base * gram


def reference(x, y, wa_words, wa_scales, wb_words, wb_scales, b, va, vb):
    R_out = core(x, y, wa_words, wa_scales, wb_words, wb_scales, b, va, vb)
    words, scales = planes(R_out)
    return R_out, words, scales

from contextlib import ExitStack

import concourse.mybir as mybir
from concourse.masks import make_identity

F32 = mybir.dt.float32
BF16 = mybir.dt.bfloat16
I32 = mybir.dt.int32
U32 = mybir.dt.uint32
U8 = mybir.dt.uint8
FP8X4 = mybir.dt.float8_e4m3fn_x4
FP4X4 = mybir.dt.float4_e2m1fn_x4
ACT = mybir.ActivationFunctionType
ALU = mybir.AluOpType

N, M, D, F = 1024, 1024, 512, 1024
P = 128
HALF = 512
FLOPS = 2 * (N * D * F + M * D * F + N * D * M + N * F * M)
SCALE = 1.0 / (32.0 * 512.0 ** 0.5)

UNITS = [
    (0, 0, 0, 0, 512), (0, 0, 1, 0, 512), (1, 0, 0, 0, 512), (1, 0, 1, 0, 512), (1, 1, 0, 0, 512), (1, 1, 1, 0, 512),
    (0, 1, 0, 0, 256), (0, 1, 1, 0, 256), (0, 1, 0, 256, 512), (0, 1, 1, 256, 512),
]
QUADS = [(0, 0), (0, 1), (1, 0), (1, 1)]
STEPS = [
    (0, 0), (0, 1), (0, 2), (0, 3), (1, 0), (1, 1), (1, 2), (1, 3),
    (2, 0), (2, 1), (3, 0), (3, 1), (2, 2), (2, 3), (3, 2), (3, 3),
]
SQUARE_ON_ACT = (4, 5, 6, 7, 8)
BASE_AT = [5, 6, 7, 8, 9, 10, 11, 12, 13, 14, 15, 16, 17, 18, 19, 20]
HAD_AT = [20, 21, 22, 23, 28, 29, 30, 31, 36, 37, 38, 39]


def tile_twotimehiddentangentkernel_x2_kernel(
    tc, x, y, wa_words, wa_scales, wb_words, wb_scales, b, va, vb, out_0, out_1, out_2
):
    nc = tc.nc
    with ExitStack() as ctx:
        keep = ctx.enter_context(tc.tile_pool(name="keep", bufs=1))
        work = ctx.enter_context(tc.tile_pool(name="work", bufs=3))
        psum = ctx.enter_context(tc.psum_pool(name="psum", bufs=1))
        ctx.enter_context(tc.manual_schedule())

        warm = keep.tile([P, 1], F32, name="warm")
        nc.vector.memset(warm[:], 0.0)
        nc.scalar.activation(out=warm[:], in_=warm[:], func=ACT.Tanh)

        ident = keep.tile([P, P], F32, name="ident", align_bytes=64)
        make_identity(nc, ident[:])

        raw = {}
        for s in (0, 1):
            for h in (0, 1):
                raw[s, h] = keep.tile([P, 4, D], BF16, name="raw_%d%d" % (s, h), align_bytes=64)

        def load_rows(s, h, j0, j1):
            src = (x, y)[s][HALF * h : HALF * (h + 1), :]
            view = src.rearrange("(p t) k -> p t k", t=4) if s == 0 else src.rearrange("(t p) k -> p t k", t=4)
            nc.sync.dma_start(out=raw[s, h][:, j0:j1, :], in_=view[:, j0:j1, :])

        w_raw = [keep.tile([P, 2 * F], U8, name="w_raw%d" % s, align_bytes=64) for s in (0, 1)]
        w_perm = [keep.tile([P, 2 * F], U8, name="w_perm%d" % s, align_bytes=64) for s in (0, 1)]
        wp_raw = [keep.tile([P, F], U8, name="wp_raw%d" % s, align_bytes=64) for s in (0, 1)]
        wp_perm = [keep.tile([P, F], U8, name="wp_perm%d" % s, align_bytes=64) for s in (0, 1)]
        for s in (0, 1):
            nc.vector.memset(wp_raw[s][:].bitcast(I32), 0)

        def load_words(s):
            nc.sync.dma_start(out=w_raw[s][:].bitcast(I32), in_=(wa_words, wb_words)[s][0].bitcast(I32))

        def load_scales(s):
            for q in range(4):
                nc.scalar.dma_start(
                    out=wp_raw[s][32 * q : 32 * q + 4, :].bitcast(I32),
                    in_=(wa_scales, wb_scales)[s][0][4 * q : 4 * q + 4, :].bitcast(I32),
                )

        vec16 = keep.tile([24, P], BF16, name="vec16")
        vec32 = keep.tile([P, P], F32, name="vec32", align_bytes=64)
        nc.vector.memset(vec32[:], 0.0)

        load_rows(0, 0, 0, 2)
        load_scales(0)
        load_words(0)
        load_rows(0, 0, 2, 4)
        for j, v in enumerate((b, va, vb)):
            nc.gpsimd.dma_start(
                out=vec16[8 * j : 8 * j + 8, :].rearrange("r (q i) -> r q i", i=8),
                in_=v.rearrange("(q r i) -> r q i", r=8, i=8),
            )
        load_rows(1, 0, 0, 4)
        load_words(1)
        load_scales(1)
        load_rows(1, 1, 0, 4)
        load_rows(0, 1, 0, 4)

        def permute(s):
            nc.vector.tensor_copy(
                out=w_perm[s][:].bitcast(I32).rearrange("p (r q i) -> p r q i", r=8, q=16),
                in_=w_raw[s][:].bitcast(I32).rearrange("p (q r i) -> p r q i", r=8, q=16),
            )
            nc.vector.tensor_copy(
                out=wp_perm[s][:].bitcast(I32).rearrange("p (r q i) -> p r q i", r=8, q=16),
                in_=wp_raw[s][:].bitcast(I32).rearrange("p (q r i) -> p r q i", r=8, q=16),
            )

        grouped, codes, planes = {}, {}, {}

        def turn(s, h, pair, on_act):
            if (s, h) not in grouped:
                grouped[s, h] = keep.tile([P, HALF, 4], BF16, name="grouped_%d%d" % (s, h), align_bytes=64)
                codes[s, h] = keep.tile([P, HALF], U32, name="codes_%d%d" % (s, h), align_bytes=64)
                planes[s, h] = keep.tile([P, HALF], U8, name="planes_%d%d" % (s, h), align_bytes=64)
            xt = psum.tile([P, 2, 2, P], F32, name="xt", tag="z", bufs=4)
            for j in (0, 1):
                words = raw[s, h][:, 2 * pair + j, :].bitcast(F32)
                for u in (0, 1):
                    nc.tensor.transpose(xt[:, j, u, :], words[:, u : D // 2 : 2], ident[:])
            flat = grouped[s, h][:].rearrange("p n t -> p (n t)")[:, 1024 * pair : 1024 * (pair + 1)]
            dst = flat.bitcast(F32).rearrange("p (j r u) -> p j r u", j=2, u=2)
            src = xt[:].rearrange("p j u r -> p j r u")
            if on_act:
                nc.scalar.copy(out=dst, in_=src)
            else:
                nc.vector.tensor_copy(out=dst, in_=src)

        def quant_in(s, h, c0, c1):
            nc.vector.quantize_mx(
                out=codes[s, h][:, c0:c1].bitcast(FP8X4),
                scales=planes[s, h][:, c0:c1],
                in_=grouped[s, h][:, c0:c1, :].rearrange("p n t -> p (n t)"),
            )

        z_tiles, t_tiles, r_tiles, d16_tiles, dq, dpl = {}, {}, {}, {}, {}, {}
        vcol = keep.tile([P, 24], F32, name="vcol")
        nvcol = keep.tile([P, 24], F32, name="nvcol")

        def z_mm(u, t):
            s, h, g, c0, c1 = UNITS[u]
            r = 4 * g + t
            z = psum.tile([P, c1 - c0], F32, name="z", tag="z", bufs=4)
            z_tiles[u, t] = z
            nc.tensor.matmul_mx(
                out=z[:],
                lhsT=w_perm[s][:, 256 * r : 256 * (r + 1)].bitcast(FP4X4),
                lhsT_scale=wp_perm[s][:, P * r : P * (r + 1)],
                rhs=codes[s, h][:, c0:c1].bitcast(FP8X4),
                rhs_scale=planes[s, h][:, c0:c1],
                start=True,
                stop=True,
            )

        def tanh(u, t):
            s, h, g, c0, c1 = UNITS[u]
            r = 4 * g + t
            if t == 0:
                t_tiles[u] = work.tile([P, 4, c1 - c0], F32, name="th", tag="th", bufs=3, align_bytes=64)
                r_tiles[u] = work.tile([P, 4, c1 - c0], F32, name="rr", tag="rr", bufs=3, align_bytes=64)
            nc.scalar.activation(
                out=t_tiles[u][:, t, :], in_=z_tiles[u, t][:], func=ACT.Tanh, bias=vcol[:, r : r + 1]
            )

        def factor(u, t):
            s, h, g = UNITS[u][:3]
            if u in SQUARE_ON_ACT:
                if t % 2 == 1:
                    nc.scalar.activation(
                        out=r_tiles[u][:, t - 1 : t + 1, :].rearrange("p t n -> p (t n)"),
                        in_=t_tiles[u][:, t - 1 : t + 1, :].rearrange("p t n -> p (t n)"),
                        func=ACT.Square,
                    )
            else:
                c = 8 * (s + 1) + 4 * g + t
                nc.vector.tensor_scalar(
                    out=r_tiles[u][:, t, :],
                    in0=t_tiles[u][:, t, :],
                    scalar1=1.0,
                    scalar2=nvcol[:, c : c + 1],
                    op0=ALU.subtract,
                    op1=ALU.mult,
                )

        def product(u, part):
            s, h, g, c0, c1 = UNITS[u]
            w = c1 - c0
            if part == 0:
                d16_tiles[u] = work.tile([P, w, 4], BF16, name="d16", tag="d16", bufs=2, align_bytes=64)
            c = slice(w // 2 * part, w // 2 * (part + 1))
            rr = r_tiles[u][:, :, c].rearrange("p t n -> p n t")
            if u in SQUARE_ON_ACT:
                col = 8 * (s + 1) + 4 * g
                nc.vector.scalar_tensor_tensor(
                    out=d16_tiles[u][:, c, :],
                    in0=rr,
                    scalar=1.0,
                    in1=nvcol[:, col : col + 4].unsqueeze(1).to_broadcast([P, w // 2, 4]),
                    op0=ALU.subtract,
                    op1=ALU.mult,
                )
            else:
                nc.vector.scalar_tensor_tensor(
                    out=d16_tiles[u][:, c, :],
                    in0=t_tiles[u][:, :, c].rearrange("p t n -> p n t"),
                    scalar=1.0,
                    in1=rr,
                    op0=ALU.add,
                    op1=ALU.mult,
                )

        def quant_d(u):
            s, h, g, c0, c1 = UNITS[u]
            if c0 == 0:
                dq[s, h, g] = keep.tile([P, HALF], U32, name="dq_%d%d%d" % (s, h, g), align_bytes=64)
                dpl[s, h, g] = keep.tile([P, HALF], U8, name="dpl_%d%d%d" % (s, h, g), align_bytes=64)
            nc.vector.quantize_mx(
                out=dq[s, h, g][:, c0:c1].bitcast(FP8X4),
                scales=dpl[s, h, g][:, c0:c1],
                in_=d16_tiles[u][:].rearrange("p n t -> p (n t)"),
            )

        gram_ps, base_sb, o_tiles, o16_tiles = {}, {}, {}, {}
        oq, opl = {}, {}

        def base(j):
            q, t = STEPS[j]
            ha, hb = QUADS[q]
            bp = psum.tile([P, HALF], F32, name="bp", tag="bp", bufs=2)
            nc.tensor.matmul_mx(
                out=bp[:],
                lhsT=codes[0, ha][:, P * t : P * (t + 1)].bitcast(FP8X4),
                lhsT_scale=planes[0, ha][:, P * t : P * (t + 1)],
                rhs=codes[1, hb][:].bitcast(FP8X4),
                rhs_scale=planes[1, hb][:],
                start=True,
                stop=True,
            )
            bs = work.tile([P, HALF], F32, name="bs", tag="bs", bufs=16, align_bytes=64)
            base_sb[j] = bs
            nc.scalar.activation(out=bs[:], in_=bp[:], func=ACT.Copy, scale=SCALE)

        def gram(j):
            q, t = STEPS[j]
            ha, hb = QUADS[q]
            if j >= 12:
                gp = psum.tile([P, HALF], F32, name="gz", tag="z", bufs=4)
            else:
                gp = psum.tile([P, HALF], F32, name="gp", tag="gp", bufs=2)
            gram_ps[j] = gp
            for g in (0, 1):
                nc.tensor.matmul_mx(
                    out=gp[:],
                    lhsT=dq[0, ha, g][:, P * t : P * (t + 1)].bitcast(FP8X4),
                    lhsT_scale=dpl[0, ha, g][:, P * t : P * (t + 1)],
                    rhs=dq[1, hb, g][:].bitcast(FP8X4),
                    rhs_scale=dpl[1, hb, g][:],
                    start=(g == 0),
                    stop=(g == 1),
                )

        def hadamard(j):
            q, t = STEPS[j]
            if t == 0:
                o_tiles[q] = work.tile([P, 4, HALF], F32, name="o32", tag="o32", bufs=3, align_bytes=64)
                o16_tiles[q] = work.tile([P, HALF, 4], BF16, name="o16", tag="o16", bufs=2, align_bytes=64)
                oq[q] = keep.tile([P, HALF], U32, name="oq%d" % q, align_bytes=64)
                opl[q] = keep.tile([P, HALF], U8, name="opl%d" % q, align_bytes=64)
            nc.vector.tensor_tensor(out=o_tiles[q][:, t, :], in0=gram_ps[j][:], in1=base_sb[j][:], op=ALU.mult)

        def store_out(q, t0, t1):
            ha, hb = QUADS[q]
            rows = out_0[HALF * ha : HALF * (ha + 1), HALF * hb : HALF * (hb + 1)]
            nc.sync.dma_start(out=rows.rearrange("(p t) m -> p t m", t=4)[:, t0:t1, :], in_=o_tiles[q][:, t0:t1, :])

        def cast(q, on_act, c0=0, c1=HALF):
            dst = o16_tiles[q][:, c0:c1, :].rearrange("p (c i) t -> p c t i", i=4)
            src = o_tiles[q][:, :, c0:c1].rearrange("p t (c i) -> p c t i", i=4)
            if on_act:
                nc.scalar.copy(out=dst, in_=src)
            else:
                nc.vector.tensor_copy(out=dst, in_=src)

        def quant_o(q, c0=0, c1=HALF):
            nc.vector.quantize_mx(
                out=oq[q][:, c0:c1].bitcast(FP8X4),
                scales=opl[q][:, c0:c1],
                in_=o16_tiles[q][:, c0:c1, :].rearrange("p n t -> p (n t)"),
            )

        def store_planes(q, c0=0, c1=HALF):
            ha, hb = QUADS[q]
            cols = slice(HALF * hb + c0, HALF * hb + c1)
            nc.sync.dma_start(
                out=out_1[ha][:, cols, :].rearrange("p m t -> p (m t)").bitcast(I32),
                in_=oq[q][:, c0:c1].bitcast(I32),
            )
            for k in range(4):
                nc.sync.dma_start(
                    out=out_2[ha][4 * k : 4 * k + 4, cols].bitcast(I32),
                    in_=opl[q][32 * k : 32 * k + 4, c0:c1].bitcast(I32),
                )

        turn(0, 0, 0, True)
        permute(0)
        turn(0, 0, 1, False)
        quant_in(0, 0, 0, 256)
        quant_in(0, 0, 256, 512)
        nc.vector.tensor_copy(out=vec32[0:24, :], in_=vec16[:])
        vps = psum.tile([P, P], F32, name="vps", tag="bp", bufs=2)
        nc.tensor.transpose(vps[:], vec32[:], ident[:])
        nc.vector.tensor_copy(out=vcol[:], in_=vps[:, 0:24])
        nc.vector.tensor_scalar(
            out=nvcol[:, 8:24], in0=vcol[:, 8:24], scalar1=-1.0, scalar2=None, op0=ALU.mult
        )

        tiles = [(u, t) for u in range(len(UNITS)) for t in range(4)]
        ahead = {"z": 0, "g": 0, "had": 0}

        def z_ahead(k):
            while ahead["z"] < min(k, len(tiles)):
                z_mm(*tiles[ahead["z"]])
                ahead["z"] += 1

        def gram_ahead(j):
            while ahead["g"] < min(j, 16):
                gram(ahead["g"])
                ahead["g"] += 1

        def next_hadamard():
            j = ahead["had"]
            hadamard(j)
            q, t = STEPS[j]
            if t % 2 == 1:
                store_out(q, t - 1, t + 1)
            ahead["had"] += 1

        for k, (u, t) in enumerate(tiles):
            z_ahead(k + 3)
            tanh(u, t)
            if k == 0:
                turn(1, 0, 0, False)
                turn(1, 0, 1, False)
                permute(1)
            if k == 1:
                quant_in(1, 0, 0, 512)
                turn(1, 1, 0, False)
            if k == 2:
                turn(1, 1, 1, False)
            if k == 3:
                quant_in(1, 1, 0, 512)
            if k == 5:
                turn(0, 1, 0, False)
            if k == 8:
                turn(0, 1, 1, False)
            if k == 10:
                quant_in(0, 1, 0, 512)
            if k > 0:
                factor(*tiles[k - 1])
            for j, at in enumerate(BASE_AT):
                if at == k:
                    base(j)
            if u > 0 and t in (1, 2):
                product(u - 1, t - 1)
            if k in HAD_AT:
                next_hadamard()
            if u > 0 and t == 3:
                quant_d(u - 1)
            if k + 1 in HAD_AT:
                gram_ahead(HAD_AT.index(k + 1) + 1)
            if k == 26:
                cast(0, True)
            if k == 29:
                quant_o(0)
                store_planes(0)
            if k == 35:
                cast(1, True)
            if k == 39:
                quant_o(1)
                store_planes(1)
        factor(*tiles[39])
        product(9, 0)
        product(9, 1)
        quant_d(9)
        for j in range(12, 16):
            gram_ahead(j + 3)
            next_hadamard()
            if j == 13:
                cast(2, True)
        quant_o(2)
        store_planes(2)
        cast(3, True, 0, 256)
        cast(3, False, 256, 512)
        quant_o(3, 256, 512)
        store_planes(3, 256, 512)
        quant_o(3, 0, 256)
        store_planes(3, 0, 256)
